import numpy as np
import ml_dtypes


def mxq(x, axis, fmt="e4m3"):
    dtype, down = {"e4m3": (ml_dtypes.float8_e4m3fn, 7), "e5m2": (ml_dtypes.float8_e5m2, 14)}[fmt]
    v = np.moveaxis(np.asarray(x, np.float32).astype(ml_dtypes.bfloat16).astype(np.float64), axis, -1)
    blocks = v.reshape(v.shape[:-1] + (-1, 32))
    amax = np.abs(blocks).max(-1, keepdims=True)
    byte = np.maximum(np.where(amax > 0, np.frexp(amax)[1] - 1 + 127, 0) - down, 1)
    scale = np.exp2(byte - 127.0)
    codes = (blocks / scale).astype(np.float32).astype(dtype).astype(np.float64)
    return np.moveaxis((codes * scale).reshape(v.shape), -1, axis)


WIDE = False


def mx_kscale(k):
    if not WIDE:
        return np.ones(k)
    levels = np.array([30, -30])
    if k % 512:
        return np.exp2(np.random.permutation(np.resize(levels, k // 32))).repeat(32)
    a = np.empty((k // 512, 16))
    for p in range(k // 512):
        a[p, :8] = np.random.permutation(np.resize(levels, 8))
        for g in range(8):
            far = levels[np.abs(levels - a[p, g]) >= 10]
            a[p, g + 8] = far[np.random.randint(len(far))]
    return np.exp2(a.ravel()).repeat(32)


def f64(x):
    return np.asarray(x).astype(np.float64)


def striped(idx):
    return np.tile(np.asarray(idx).reshape(-1, 16).T, (8, 1)).astype(np.uint16)


def unstriped(offs):
    return offs[:16].T.reshape(-1).astype(np.int64)


E2M1 = np.array([0.0, 0.5, 1.0, 1.5, 2.0, 3.0, 4.0, 6.0, -0.0, -0.5, -1.0, -1.5, -2.0, -3.0, -4.0, -6.0])


def pack_weight(w, fmt):
    k, n = w.shape
    w = f64(np.asarray(w, np.float32).astype(ml_dtypes.bfloat16)).reshape(k // 32, 32, n)
    amax = np.abs(w).max(1)
    if fmt in ("e4m3", "e5m2"):
        byte = np.frexp(amax)[1] - 1 + 127 - (7 if fmt == "e4m3" else 14)
    else:
        mant, ex = np.frexp(amax / 6.0)
        byte = np.where(mant > 0.5, ex, ex - 1) + 127
    byte = np.clip(np.where(amax > 0, byte, 1), 1, 254)
    scaled = (w * np.exp2(127.0 - byte)[:, None, :]).reshape(k, n).astype(np.float32)
    by_word = np.ascontiguousarray(scaled.reshape(k // 512, 128, 4, n).transpose(0, 1, 3, 2))
    if fmt in ("e4m3", "e5m2"):
        words = by_word.astype(ml_dtypes.float8_e4m3fn if fmt == "e4m3" else ml_dtypes.float8_e5m2).view(np.uint8)
    else:
        c = by_word.astype(ml_dtypes.float4_e2m1fn).view(np.uint8) & 0xF
        words = (c[..., 0::2] | (c[..., 1::2] << 4)).reshape(k // 512, 128, 2 * n)
    return np.ascontiguousarray(words), np.ascontiguousarray(byte.astype(np.uint8).reshape(k // 512, 16, n))


def unpack_weight(words, scales, fmt):
    g, _, n = scales.shape
    words = np.ascontiguousarray(words).reshape(g, 128, n, -1)
    if fmt in ("e4m3", "e5m2"):
        vals = words.view(ml_dtypes.float8_e4m3fn if fmt == "e4m3" else ml_dtypes.float8_e5m2).astype(np.float64)
    else:
        nib = np.empty((g, 128, n, 4), np.uint8)
        nib[..., 0::2] = words & 0xF
        nib[..., 1::2] = words >> 4
        vals = E2M1[nib]
    vals = vals * np.repeat(np.exp2(scales.astype(np.float64) - 127.0), 8, axis=1)[..., None]
    return vals.transpose(0, 1, 3, 2).reshape(g * 512, n)


K, T, J, R, N, S = 512, 1024, 256, 512, 256, 1024


def setup_inputs():
    n = np.random.standard_normal
    idx = np.random.permutation(T)[:J]
    idx2 = np.random.permutation(T)[:J]
    idx3 = np.random.permutation(J)[:J]
    idx4 = np.random.permutation(S)[:N]
    fk = mx_kscale(K)
    fr = mx_kscale(R)
    wp = pack_weight(n((K, R)) * 1 / np.sqrt(K) / fk[:, None] * fr, "e5m2")
    vsp = pack_weight(n((R, S)) * 1 / np.sqrt(R) / fr[:, None], "e4m3")
    return {
        "cq": (np.random.randint(-7, 8, (K, T)).astype(np.float64)).astype(np.float32),
        "ga": (np.random.uniform(0.1, 0.4, (K, 1)) * fk[:, None]).astype(np.float32),
        "gb": (np.random.uniform(0.1, 0.4, (K, 1)) * fk[:, None]).astype(np.float32),
        "w_words": wp[0],
        "w_scales": wp[1],
        "sa": (np.random.uniform(0.5, 1.6, (R, 1))).astype(np.float32),
        "vs_words": vsp[0],
        "vs_scales": vsp[1],
        "offs": striped(idx),
        "offs2": striped(idx2),
        "offs3": striped(idx3),
        "offs4": striped(idx4),
    }


def reference(cq, ga, gb, w_words, w_scales, sa, vs_words, vs_scales, offs, offs2, offs3, offs4):
    idx = unstriped(offs)
    idx2 = unstriped(offs2)
    idx3 = unstriped(offs3)
    idx4 = unstriped(offs4)
    wu = unpack_weight(w_words, w_scales, "e5m2")
    vsu = unpack_weight(vs_words, vs_scales, "e4m3")
    x1 = f64(cq)[:, idx] * f64(ga)
    x2 = f64(cq)[:, idx2] * f64(gb)
    x1q = mxq(x1, 0, "e4m3")
    a = wu.T @ x1q
    x2q = mxq(x2, 0, "e4m3")
    b = wu.T @ x2q
    hid = np.abs(a - b[:, idx3] * f64(sa))
    vsidx4g = vsu[:, idx4]
    hidq = mxq(hid, 0, "e5m2")
    y = vsidx4g.T @ hidq
    return y

@@ -1,0 +1,200 @@
+from contextlib import ExitStack
+
+import concourse.mybir as mybir
+
+K, T, J, R, N, S = 512, 1024, 256, 512, 256, 1024
+FLOPS = 2 * K * R * J * 2 + 2 * R * N * J
+
+F32 = mybir.dt.float32
+BF16 = mybir.dt.bfloat16
+I32 = mybir.dt.int32
+U32 = mybir.dt.uint32
+U16 = mybir.dt.uint16
+U8 = mybir.dt.uint8
+E4M3X4 = mybir.dt.float8_e4m3fn_x4
+E5M2X4 = mybir.dt.float8_e5m2_x4
+ACT = mybir.ActivationFunctionType
+ALU = mybir.AluOpType
+
+P = 128
+PACK = 4
+HALF = J // 2
+LIST_COLS = J // 16
+
+
+def tile_list_scaledpartner_twosteps_store_plain_kernel(
+    tc, cq, ga, gb, w_words, w_scales, sa, vs_words, vs_scales, offs, offs2, offs3, offs4, out
+):
+    nc = tc.nc
+    with ExitStack() as ctx:
+        sb = ctx.enter_context(tc.tile_pool(name="sb", bufs=1))
+        psum = ctx.enter_context(tc.psum_pool(name="psum", bufs=1))
+
+        def load_list(name, src):
+            tile = sb.tile([P, LIST_COLS], U16, name=name)
+            nc.sync.dma_start(out=tile[:], in_=src)
+            return tile
+
+        def load_row_factors(name, src, queue):
+            tile = sb.tile([P, PACK], F32, name=name)
+            queue.dma_start(out=tile[:], in_=src.rearrange("(p t) o -> p (t o)", t=PACK))
+            return tile
+
+        def load_words(name, src, width):
+            tile = sb.tile([P, width], I32, name=name, align_bytes=64)
+            nc.sync.dma_start(out=tile[:], in_=src[0].rearrange("p c t -> p (c t)").bitcast(I32))
+            return tile
+
+        def load_scale_plane(name, src, width):
+            staged = sb.tile([4, 4, width // 4], I32, name=name + "_staged")
+            nc.gpsimd.dma_start(out=staged[:], in_=src[0].bitcast(I32).rearrange("(q r) c -> r q c", r=4))
+            plane = sb.tile([P, width // 4], I32, name=name, align_bytes=64)
+            nc.vector.memset(plane[:], 0)
+            for q in range(4):
+                nc.vector.tensor_copy(out=plane[32 * q : 32 * q + 4, :], in_=staged[:, q, :])
+            return plane
+
+        cq_rows = cq.rearrange("(p t) c -> p t c", t=PACK)
+        cq_sb = [sb.tile([P, T], F32, name="cq%d" % t) for t in range(PACK)]
+
+        nc.sync.dma_start(out=cq_sb[0][:], in_=cq_rows[:, 0, :])
+        list2 = load_list("list2", offs2)
+        list1 = load_list("list1", offs)
+        gb_sb = load_row_factors("gb_sb", gb, nc.scalar)
+        ga_sb = load_row_factors("ga_sb", ga, nc.scalar)
+        nc.sync.dma_start(out=cq_sb[1][:], in_=cq_rows[:, 1, :])
+        nc.sync.dma_start(out=cq_sb[2][:], in_=cq_rows[:, 2, :])
+        w_raw = load_words("w_raw", w_words, R)
+        nc.sync.dma_start(out=cq_sb[3][:], in_=cq_rows[:, 3, :])
+        list4 = load_list("list4", offs4)
+        list3 = load_list("list3", offs3)
+        vs_all = load_words("vs_all", vs_words, S)
+        w_plane_raw = load_scale_plane("w_plane_raw", w_scales, R)
+        vs_plane_all = load_scale_plane("vs_plane_all", vs_scales, S)
+        sa_sb = load_row_factors("sa_sb", sa, nc.gpsimd)
+
+        w_plane = sb.tile([P, R], U8, name="w_plane", align_bytes=64)
+        nc.vector.tensor_copy(
+            out=w_plane[:].rearrange("p (t c i) -> p c t i", t=PACK, i=16),
+            in_=w_plane_raw[:].bitcast(U8).rearrange("p (c i t) -> p c t i", t=PACK, i=16),
+        )
+        w_codes = sb.tile([P, R], I32, name="w_codes", align_bytes=64)
+        nc.vector.tensor_copy(
+            out=w_codes[:].rearrange("p (t c i) -> p c t i", t=PACK, i=4),
+            in_=w_raw[:].rearrange("p (c i t) -> p c t i", t=PACK, i=4),
+        )
+        vs_plane = sb.tile([P, N], U8, name="vs_plane", align_bytes=64)
+        nc.vector.tensor_copy(out=vs_plane[:], in_=vs_plane_all[:].bitcast(U8).indirect(list4[:]))
+
+        x1_rows = sb.tile([P, PACK, J], BF16, name="x1_rows")
+        x2_rows = sb.tile([P, PACK, J], BF16, name="x2_rows")
+        for t in range(PACK):
+            for rows, picks, step in ((x2_rows, list2, gb_sb), (x1_rows, list1, ga_sb)):
+                nc.scalar.activation(
+                    out=rows[:, t, :], in_=cq_sb[t][:].indirect(picks[:]), func=ACT.Copy, scale=step[:, t : t + 1]
+                )
+
+        def quantise_x(name, rows):
+            woven = sb.tile([P, J * PACK], BF16, name=name + "_woven", align_bytes=64)
+            nc.vector.tensor_copy(
+                out=woven[:].rearrange("p (c i t) -> p c t i", t=PACK, i=4),
+                in_=rows[:].rearrange("p t (c i) -> p c t i", i=4),
+            )
+            codes = sb.tile([P, J], U32, name=name + "_codes", align_bytes=64)
+            plane = sb.tile([P, J], U8, name=name + "_plane", align_bytes=64)
+            nc.vector.quantize_mx(out=codes[:].bitcast(E4M3X4), scales=plane[:], in_=woven[:])
+            return codes, plane
+
+        def times_w(acc, t, codes, plane):
+            cols = slice(P * t, P * (t + 1))
+            nc.tensor.matmul_mx(
+                out=acc,
+                lhsT=w_codes[:, cols].bitcast(E5M2X4),
+                lhsT_scale=w_plane[:, cols],
+                rhs=codes.bitcast(E4M3X4),
+                rhs_scale=plane,
+                start=True,
+                stop=True,
+            )
+
+        x2_codes, x2_plane = quantise_x("x2", x2_rows)
+        b_sb = []
+        for t in range(PACK):
+            b_ps = psum.tile([P, J], F32, name="b_ps%d" % t, tag="bank%d" % t)
+            times_w(b_ps[:], t, x2_codes[:], x2_plane[:])
+            b_t = sb.tile([P, J], F32, name="b_sb%d" % t)
+            if t == 0:
+                nc.scalar.copy(out=b_t[:], in_=b_ps[:])
+            else:
+                nc.vector.tensor_copy(out=b_t[:], in_=b_ps[:])
+            b_sb.append(b_t)
+
+        x1_codes, x1_plane = quantise_x("x1", x1_rows)
+        a_ps = []
+        for h in range(2):
+            cols = slice(HALF * h, HALF * (h + 1))
+            a_h = psum.tile([P, PACK, HALF], F32, name="a_ps%d" % h)
+            for t in range(PACK):
+                times_w(a_h[:, t, :], t, x1_codes[:, cols], x1_plane[:, cols])
+            a_ps.append(a_h)
+
+        vs_codes = sb.tile([P, N], U32, name="vs_codes", align_bytes=64)
+        nc.vector.tensor_copy(out=vs_codes[:], in_=vs_all[:].bitcast(U32).indirect(list4[:]))
+
+        for h in range(2):
+            partner = sb.tile([P, PACK, HALF], F32, name="partner%d" % h)
+            for t in range(PACK):
+                nc.scalar.activation(
+                    out=partner[:, t, :],
+                    in_=b_sb[t][:].indirect(list3[:, 8 * h : 8 * (h + 1)]),
+                    func=ACT.Copy,
+                    scale=sa_sb[:, t : t + 1],
+                )
+            hid = sb.tile([P, HALF * PACK], BF16, name="hid%d" % h, align_bytes=64)
+            diff = sb.tile([P, HALF * PACK], F32, name="diff%d" % h)
+            if h == 0:
+                nc.vector.tensor_tensor(
+                    out=diff[:].rearrange("p (c i t) -> p c t i", t=PACK, i=4),
+                    in0=a_ps[h][:].rearrange("p t (c i) -> p c t i", i=4),
+                    in1=partner[:].rearrange("p t (c i) -> p c t i", i=4),
+                    op=ALU.subtract,
+                )
+                nc.vector.scalar_tensor_tensor(
+                    out=hid[:], in0=diff[:], scalar=-1.0, in1=diff[:], op0=ALU.mult, op1=ALU.max
+                )
+            else:
+                for t in range(PACK):
+                    nc.vector.tensor_tensor(
+                        out=diff[:, HALF * t : HALF * (t + 1)],
+                        in0=a_ps[h][:, t, :],
+                        in1=partner[:, t, :],
+                        op=ALU.subtract,
+                    )
+                nc.scalar.activation(
+                    out=hid[:].rearrange("p (j t) -> p j t", t=PACK),
+                    in_=diff[:].rearrange("p (t j) -> p j t", t=PACK),
+                    func=ACT.Abs,
+                )
+            hid_codes = sb.tile([P, HALF], U32, name="hid_codes%d" % h, align_bytes=64)
+            hid_plane = sb.tile([P, HALF], U8, name="hid_plane%d" % h, align_bytes=64)
+            nc.vector.quantize_mx(out=hid_codes[:].bitcast(E5M2X4), scales=hid_plane[:], in_=hid[:])
+            for m in range(2):
+                rows = slice(P * m, P * (m + 1))
+                y_ps = psum.tile([P, HALF], F32, name="y_ps%d%d" % (h, m), tag="bank%d" % (2 * h + m))
+                nc.tensor.matmul_mx(
+                    out=y_ps[:],
+                    lhsT=vs_codes[:, rows].bitcast(E4M3X4),
+                    lhsT_scale=vs_plane[:, rows],
+                    rhs=hid_codes[:].bitcast(E5M2X4),
+                    rhs_scale=hid_plane[:],
+                    start=True,
+                    stop=True,
+                )
+                y_sb = sb.tile([P, HALF], F32, name="y_sb%d%d" % (h, m))
+                dst = out[rows, HALF * h : HALF * (h + 1)]
+                if m == 0:
+                    nc.vector.tensor_copy(out=y_sb[:], in_=y_ps[:])
+                    nc.sync.dma_start(out=dst, in_=y_sb[:])
+                else:
+                    nc.scalar.copy(out=y_sb[:], in_=y_ps[:])
+                    nc.scalar.dma_start(out=dst, in_=y_sb[:])

@@ -28,6 +28,7 @@ def tile_list_scaledpartner_twosteps_store_plain_kernel(
     nc = tc.nc
     with ExitStack() as ctx:
         sb = ctx.enter_context(tc.tile_pool(name="sb", bufs=1))
+        shared = ctx.enter_context(tc.tile_pool(name="shared", bufs=1))
         psum = ctx.enter_context(tc.psum_pool(name="psum", bufs=1))
 
         def load_list(name, src):
@@ -35,24 +36,13 @@ def tile_list_scaledpartner_twosteps_store_plain_kernel(
             nc.sync.dma_start(out=tile[:], in_=src)
             return tile
 
-        def load_row_factors(name, src, queue):
-            tile = sb.tile([P, PACK], F32, name=name)
-            queue.dma_start(out=tile[:], in_=src.rearrange("(p t) o -> p (t o)", t=PACK))
+        def load_row_factors(name, src, queue, lo=0, hi=PACK):
+            tile = sb.tile([P, hi - lo], F32, name=name)
+            queue.dma_start(out=tile[:], in_=src.rearrange("(p t) o -> p (t o)", t=PACK)[:, lo:hi])
             return tile
 
-        def load_words(name, src, width):
-            tile = sb.tile([P, width], I32, name=name, align_bytes=64)
+        def load_words(tile, src):
             nc.sync.dma_start(out=tile[:], in_=src[0].rearrange("p c t -> p (c t)").bitcast(I32))
-            return tile
-
-        def load_scale_plane(name, src, width):
-            staged = sb.tile([4, 4, width // 4], I32, name=name + "_staged")
-            nc.gpsimd.dma_start(out=staged[:], in_=src[0].bitcast(I32).rearrange("(q r) c -> r q c", r=4))
-            plane = sb.tile([P, width // 4], I32, name=name, align_bytes=64)
-            nc.vector.memset(plane[:], 0)
-            for q in range(4):
-                nc.vector.tensor_copy(out=plane[32 * q : 32 * q + 4, :], in_=staged[:, q, :])
-            return plane
 
         cq_rows = cq.rearrange("(p t) c -> p t c", t=PACK)
         cq_sb = [sb.tile([P, T], F32, name="cq%d" % t) for t in range(PACK)]
@@ -61,49 +51,71 @@ def tile_list_scaledpartner_twosteps_store_plain_kernel(
         list2 = load_list("list2", offs2)
         list1 = load_list("list1", offs)
         gb_sb = load_row_factors("gb_sb", gb, nc.scalar)
-        ga_sb = load_row_factors("ga_sb", ga, nc.scalar)
+        ga_early = load_row_factors("ga_early", ga, nc.scalar, 0, 2)
+        w_staged = sb.tile([4, 4, R // 4], I32, name="w_staged")
+        nc.scalar.dma_start(out=w_staged[:], in_=w_scales[0].bitcast(I32).rearrange("(q r) c -> r q c", r=4))
         nc.sync.dma_start(out=cq_sb[1][:], in_=cq_rows[:, 1, :])
         nc.sync.dma_start(out=cq_sb[2][:], in_=cq_rows[:, 2, :])
-        w_raw = load_words("w_raw", w_words, R)
         nc.sync.dma_start(out=cq_sb[3][:], in_=cq_rows[:, 3, :])
-        list4 = load_list("list4", offs4)
+        ga_late = load_row_factors("ga_late", ga, nc.sync, 2, 4)
+        w_raw = sb.tile([P, R], I32, name="w_raw")
+        load_words(w_raw, w_words)
         list3 = load_list("list3", offs3)
-        vs_all = load_words("vs_all", vs_words, S)
-        w_plane_raw = load_scale_plane("w_plane_raw", w_scales, R)
-        vs_plane_all = load_scale_plane("vs_plane_all", vs_scales, S)
-        sa_sb = load_row_factors("sa_sb", sa, nc.gpsimd)
+        sa_sb = load_row_factors("sa_sb", sa, nc.sync)
+        w_plane_raw = sb.tile([P, R // 4], I32, name="w_plane_raw")
+        nc.vector.memset(w_plane_raw[:], 0)
+        vs_all = shared.tile([P, S], I32, name="vs_all", offset=0)
+        vs_plane_all = shared.tile([P, S // 4], I32, name="vs_plane_all", offset=4 * S)
+        nc.vector.memset(vs_plane_all[:], 0)
+        load_words(vs_all, vs_words)
+        for q in range(4):
+            nc.sync.dma_start(out=vs_plane_all[32 * q : 32 * q + 4, :], in_=vs_scales[0, 4 * q : 4 * q + 4, :].bitcast(I32))
+        list4 = load_list("list4", offs4)
+        for q in range(4):
+            nc.vector.tensor_copy(out=w_plane_raw[32 * q : 32 * q + 4, :], in_=w_staged[:, q, :])
 
         w_plane = sb.tile([P, R], U8, name="w_plane", align_bytes=64)
         nc.vector.tensor_copy(
             out=w_plane[:].rearrange("p (t c i) -> p c t i", t=PACK, i=16),
             in_=w_plane_raw[:].bitcast(U8).rearrange("p (c i t) -> p c t i", t=PACK, i=16),
         )
-        w_codes = sb.tile([P, R], I32, name="w_codes", align_bytes=64)
+
+        x1_rows = sb.tile([P, PACK, J], BF16, name="x1_rows")
+        x2_rows = sb.tile([P, PACK, J], BF16, name="x2_rows")
+        x1_woven = sb.tile([P, J, PACK], BF16, name="x1_woven", align_bytes=64)
+        x2_woven = sb.tile([P, J, PACK], BF16, name="x2_woven", align_bytes=64)
+
+        def fetch(rows, t, picks, step):
+            nc.scalar.activation(out=rows[:, t, :], in_=cq_sb[t][:].indirect(picks[:]), func=ACT.Copy, scale=step)
+
+        def weave(woven, rows, t0):
+            nc.vector.tensor_copy(
+                out=woven[:, :, t0 : t0 + 2], in_=rows[:, t0 : t0 + 2, :].rearrange("p t j -> p j t")
+            )
+
+        def quantise_x(name, woven):
+            codes = sb.tile([P, J], U32, name=name + "_codes", align_bytes=64)
+            plane = sb.tile([P, J], U8, name=name + "_plane", align_bytes=64)
+            nc.vector.quantize_mx(
+                out=codes[:].bitcast(E4M3X4), scales=plane[:], in_=woven[:].rearrange("p j t -> p (j t)")
+            )
+            return codes, plane
+
+        for t in range(2):
+            fetch(x2_rows, t, list2, gb_sb[:, t : t + 1])
+            fetch(x1_rows, t, list1, ga_early[:, t : t + 1])
+        weave(x2_woven, x2_rows, 0)
+        weave(x1_woven, x1_rows, 0)
+        for t in range(2, 4):
+            fetch(x2_rows, t, list2, gb_sb[:, t : t + 1])
+        for t in range(2, 4):
+            fetch(x1_rows, t, list1, ga_late[:, t - 2 : t - 1])
+        weave(x2_woven, x2_rows, 2)
+        w_codes = sb.tile([P, R], I32, name="w_codes", tag="w_codes", align_bytes=64)
         nc.vector.tensor_copy(
             out=w_codes[:].rearrange("p (t c i) -> p c t i", t=PACK, i=4),
             in_=w_raw[:].rearrange("p (c i t) -> p c t i", t=PACK, i=4),
         )
-        vs_plane = sb.tile([P, N], U8, name="vs_plane", align_bytes=64)
-        nc.vector.tensor_copy(out=vs_plane[:], in_=vs_plane_all[:].bitcast(U8).indirect(list4[:]))
-
-        x1_rows = sb.tile([P, PACK, J], BF16, name="x1_rows")
-        x2_rows = sb.tile([P, PACK, J], BF16, name="x2_rows")
-        for t in range(PACK):
-            for rows, picks, step in ((x2_rows, list2, gb_sb), (x1_rows, list1, ga_sb)):
-                nc.scalar.activation(
-                    out=rows[:, t, :], in_=cq_sb[t][:].indirect(picks[:]), func=ACT.Copy, scale=step[:, t : t + 1]
-                )
-
-        def quantise_x(name, rows):
-            woven = sb.tile([P, J * PACK], BF16, name=name + "_woven", align_bytes=64)
-            nc.vector.tensor_copy(
-                out=woven[:].rearrange("p (c i t) -> p c t i", t=PACK, i=4),
-                in_=rows[:].rearrange("p t (c i) -> p c t i", i=4),
-            )
-            codes = sb.tile([P, J], U32, name=name + "_codes", align_bytes=64)
-            plane = sb.tile([P, J], U8, name=name + "_plane", align_bytes=64)
-            nc.vector.quantize_mx(out=codes[:].bitcast(E4M3X4), scales=plane[:], in_=woven[:])
-            return codes, plane
 
         def times_w(acc, t, codes, plane):
             cols = slice(P * t, P * (t + 1))
@@ -117,7 +129,9 @@ def tile_list_scaledpartner_twosteps_store_plain_kernel(
                 stop=True,
             )
 
-        x2_codes, x2_plane = quantise_x("x2", x2_rows)
+        x2_codes, x2_plane = quantise_x("x2", x2_woven)
+        weave(x1_woven, x1_rows, 2)
+        x1_codes, x1_plane = quantise_x("x1", x1_woven)
         b_sb = []
         for t in range(PACK):
             b_ps = psum.tile([P, J], F32, name="b_ps%d" % t, tag="bank%d" % t)
@@ -129,7 +143,6 @@ def tile_list_scaledpartner_twosteps_store_plain_kernel(
                 nc.vector.tensor_copy(out=b_t[:], in_=b_ps[:])
             b_sb.append(b_t)
 
-        x1_codes, x1_plane = quantise_x("x1", x1_rows)
         a_ps = []
         for h in range(2):
             cols = slice(HALF * h, HALF * (h + 1))
@@ -138,11 +151,13 @@ def tile_list_scaledpartner_twosteps_store_plain_kernel(
                 times_w(a_h[:, t, :], t, x1_codes[:, cols], x1_plane[:, cols])
             a_ps.append(a_h)
 
+        vs_plane = sb.tile([P, N], U8, name="vs_plane", align_bytes=64)
+        nc.vector.tensor_copy(out=vs_plane[:], in_=vs_plane_all[:].bitcast(U8).indirect(list4[:]))
         vs_codes = sb.tile([P, N], U32, name="vs_codes", align_bytes=64)
         nc.vector.tensor_copy(out=vs_codes[:], in_=vs_all[:].bitcast(U32).indirect(list4[:]))
 
         for h in range(2):
-            partner = sb.tile([P, PACK, HALF], F32, name="partner%d" % h)
+            partner = sb.tile([P, PACK, HALF], F32, name="partner%d" % h, tag=("partner", "w_codes")[h], align_bytes=64)
             for t in range(PACK):
                 nc.scalar.activation(
                     out=partner[:, t, :],
@@ -151,7 +166,7 @@ def tile_list_scaledpartner_twosteps_store_plain_kernel(
                     scale=sa_sb[:, t : t + 1],
                 )
             hid = sb.tile([P, HALF * PACK], BF16, name="hid%d" % h, align_bytes=64)
-            diff = sb.tile([P, HALF * PACK], F32, name="diff%d" % h)
+            diff = shared.tile([P, HALF * PACK], F32, name="diff%d" % h, offset=(3072, 1024)[h])
             if h == 0:
                 nc.vector.tensor_tensor(
                     out=diff[:].rearrange("p (c i t) -> p c t i", t=PACK, i=4),
@@ -159,9 +174,7 @@ def tile_list_scaledpartner_twosteps_store_plain_kernel(
                     in1=partner[:].rearrange("p t (c i) -> p c t i", i=4),
                     op=ALU.subtract,
                 )
-                nc.vector.scalar_tensor_tensor(
-                    out=hid[:], in0=diff[:], scalar=-1.0, in1=diff[:], op0=ALU.mult, op1=ALU.max
-                )
+                nc.scalar.activation(out=hid[:], in_=diff[:], func=ACT.Abs)
             else:
                 for t in range(PACK):
                     nc.vector.tensor_tensor(

@@ -54,6 +54,10 @@ def tile_list_scaledpartner_twosteps_store_plain_kernel(
         ga_early = load_row_factors("ga_early", ga, nc.scalar, 0, 2)
         w_staged = sb.tile([4, 4, R // 4], I32, name="w_staged")
         nc.scalar.dma_start(out=w_staged[:], in_=w_scales[0].bitcast(I32).rearrange("(q r) c -> r q c", r=4))
+        warm_in = sb.tile([P, 1], F32, name="warm_in")
+        nc.gpsimd.memset(warm_in[:], 0.0)
+        warm_out = sb.tile([P, 1], F32, name="warm_out")
+        nc.scalar.activation(out=warm_out[:], in_=warm_in[:], func=ACT.Abs)
         nc.sync.dma_start(out=cq_sb[1][:], in_=cq_rows[:, 1, :])
         nc.sync.dma_start(out=cq_sb[2][:], in_=cq_rows[:, 2, :])
         nc.sync.dma_start(out=cq_sb[3][:], in_=cq_rows[:, 3, :])

@@ -64,17 +64,17 @@ def tile_list_scaledpartner_twosteps_store_plain_kernel(
         ga_late = load_row_factors("ga_late", ga, nc.sync, 2, 4)
         w_raw = sb.tile([P, R], I32, name="w_raw")
         load_words(w_raw, w_words)
-        list3 = load_list("list3", offs3)
-        sa_sb = load_row_factors("sa_sb", sa, nc.sync)
         w_plane_raw = sb.tile([P, R // 4], I32, name="w_plane_raw")
         nc.vector.memset(w_plane_raw[:], 0)
         vs_all = shared.tile([P, S], I32, name="vs_all", offset=0)
-        vs_plane_all = shared.tile([P, S // 4], I32, name="vs_plane_all", offset=4 * S)
+        vs_plane_all = sb.tile([P, S // 4], I32, name="vs_plane_all")
         nc.vector.memset(vs_plane_all[:], 0)
+        list4 = load_list("list4", offs4)
         load_words(vs_all, vs_words)
         for q in range(4):
             nc.sync.dma_start(out=vs_plane_all[32 * q : 32 * q + 4, :], in_=vs_scales[0, 4 * q : 4 * q + 4, :].bitcast(I32))
-        list4 = load_list("list4", offs4)
+        list3 = load_list("list3", offs3)
+        sa_sb = load_row_factors("sa_sb", sa, nc.sync)
         for q in range(4):
             nc.vector.tensor_copy(out=w_plane_raw[32 * q : 32 * q + 4, :], in_=w_staged[:, q, :])
 
@@ -86,40 +86,45 @@ def tile_list_scaledpartner_twosteps_store_plain_kernel(
 
         x1_rows = sb.tile([P, PACK, J], BF16, name="x1_rows")
         x2_rows = sb.tile([P, PACK, J], BF16, name="x2_rows")
-        x1_woven = sb.tile([P, J, PACK], BF16, name="x1_woven", align_bytes=64)
+        x1_woven = shared.tile([P, J, PACK], BF16, name="x1_woven", align_bytes=64, offset=5120)
         x2_woven = sb.tile([P, J, PACK], BF16, name="x2_woven", align_bytes=64)
 
         def fetch(rows, t, picks, step):
             nc.scalar.activation(out=rows[:, t, :], in_=cq_sb[t][:].indirect(picks[:]), func=ACT.Copy, scale=step)
 
-        def weave(woven, rows, t0):
-            nc.vector.tensor_copy(
-                out=woven[:, :, t0 : t0 + 2], in_=rows[:, t0 : t0 + 2, :].rearrange("p t j -> p j t")
+        def weave(move, woven, rows, t0, cols):
+            move(
+                out=woven[:, cols, t0 : t0 + 2], in_=rows[:, t0 : t0 + 2, cols].rearrange("p t j -> p j t")
             )
 
-        def quantise_x(name, woven):
-            codes = sb.tile([P, J], U32, name=name + "_codes", align_bytes=64)
-            plane = sb.tile([P, J], U8, name=name + "_plane", align_bytes=64)
+        def quantise(woven, codes, plane, cols, fmt):
             nc.vector.quantize_mx(
-                out=codes[:].bitcast(E4M3X4), scales=plane[:], in_=woven[:].rearrange("p j t -> p (j t)")
+                out=codes[:, cols].bitcast(fmt), scales=plane[:, cols], in_=woven[:, cols, :].rearrange("p j t -> p (j t)")
             )
+
+        def mx_tiles(name, width):
+            codes = sb.tile([P, width], U32, name=name + "_codes", align_bytes=64)
+            plane = sb.tile([P, width], U8, name=name + "_plane", align_bytes=64)
             return codes, plane
 
+        halves = [slice(HALF * h, HALF * (h + 1)) for h in range(2)]
+        all_slots = slice(0, J)
         for t in range(2):
             fetch(x2_rows, t, list2, gb_sb[:, t : t + 1])
             fetch(x1_rows, t, list1, ga_early[:, t : t + 1])
-        weave(x2_woven, x2_rows, 0)
-        weave(x1_woven, x1_rows, 0)
+        weave(nc.vector.tensor_copy, x2_woven, x2_rows, 0, all_slots)
+        weave(nc.vector.tensor_copy, x1_woven, x1_rows, 0, all_slots)
         for t in range(2, 4):
             fetch(x2_rows, t, list2, gb_sb[:, t : t + 1])
         for t in range(2, 4):
             fetch(x1_rows, t, list1, ga_late[:, t - 2 : t - 1])
-        weave(x2_woven, x2_rows, 2)
         w_codes = sb.tile([P, R], I32, name="w_codes", tag="w_codes", align_bytes=64)
-        nc.vector.tensor_copy(
-            out=w_codes[:].rearrange("p (t c i) -> p c t i", t=PACK, i=4),
-            in_=w_raw[:].rearrange("p (c i t) -> p c t i", t=PACK, i=4),
-        )
+
+        def deal_w(lo, hi):
+            nc.vector.tensor_copy(
+                out=w_codes[:].rearrange("p (t c i) -> p c t i", t=PACK, i=4)[:, :, lo:hi, :],
+                in_=w_raw[:].rearrange("p (c i t) -> p c t i", t=PACK, i=4)[:, :, lo:hi, :],
+            )
 
         def times_w(acc, t, codes, plane):
             cols = slice(P * t, P * (t + 1))
@@ -133,68 +138,75 @@ def tile_list_scaledpartner_twosteps_store_plain_kernel(
                 stop=True,
             )
 
-        x2_codes, x2_plane = quantise_x("x2", x2_woven)
-        weave(x1_woven, x1_rows, 2)
-        x1_codes, x1_plane = quantise_x("x1", x1_woven)
+        x2_codes, x2_plane = mx_tiles("x2", J)
+        for cols in halves:
+            weave(nc.vector.tensor_copy, x2_woven, x2_rows, 2, cols)
+        deal_w(0, 1)
+        for cols in halves:
+            quantise(x2_woven, x2_codes, x2_plane, cols, E4M3X4)
+        deal_w(1, PACK)
+
+        vs_codes = sb.tile([P, N], U32, name="vs_codes", align_bytes=64)
+        nc.vector.tensor_copy(out=vs_codes[:], in_=vs_all[:].bitcast(U32).indirect(list4[:]))
+        vs_plane = sb.tile([P, N], U8, name="vs_plane", align_bytes=64)
+        nc.vector.tensor_copy(out=vs_plane[:], in_=vs_plane_all[:].bitcast(U8).indirect(list4[:]))
+
+        weave(nc.scalar.copy, x1_woven, x1_rows, 2, halves[0])
+        weave(nc.vector.tensor_copy, x1_woven, x1_rows, 2, halves[1])
+        x1_codes = shared.tile([P, J], U32, name="x1_codes", align_bytes=64, offset=0)
+        x1_plane = sb.tile([P, J], U8, name="x1_plane", align_bytes=64)
+
         b_sb = []
         for t in range(PACK):
             b_ps = psum.tile([P, J], F32, name="b_ps%d" % t, tag="bank%d" % t)
-            times_w(b_ps[:], t, x2_codes[:], x2_plane[:])
-            b_t = sb.tile([P, J], F32, name="b_sb%d" % t)
+            for cols in halves:
+                times_w(b_ps[:, cols], t, x2_codes[:, cols], x2_plane[:, cols])
+            b_t = shared.tile([P, J if t == PACK - 1 else 2 * J], F32, name="b_sb%d" % t, offset=(8192, 3072, 6144, 1024)[t])
             if t == 0:
-                nc.scalar.copy(out=b_t[:], in_=b_ps[:])
+                nc.scalar.copy(out=b_t[:, 0:J], in_=b_ps[:])
             else:
-                nc.vector.tensor_copy(out=b_t[:], in_=b_ps[:])
+                nc.vector.tensor_copy(out=b_t[:, 0:J], in_=b_ps[:])
+            if t == 1:
+                quantise(x1_woven, x1_codes, x1_plane, all_slots, E4M3X4)
             b_sb.append(b_t)
 
-        a_ps = []
-        for h in range(2):
-            cols = slice(HALF * h, HALF * (h + 1))
-            a_h = psum.tile([P, PACK, HALF], F32, name="a_ps%d" % h)
-            for t in range(PACK):
-                times_w(a_h[:, t, :], t, x1_codes[:, cols], x1_plane[:, cols])
-            a_ps.append(a_h)
+        a_ps = [psum.tile([P, J], F32, name="a_ps%d" % t) for t in range(PACK)]
+        for t in range(PACK):
+            times_w(a_ps[t][:], t, x1_codes[:], x1_plane[:])
 
-        vs_plane = sb.tile([P, N], U8, name="vs_plane", align_bytes=64)
-        nc.vector.tensor_copy(out=vs_plane[:], in_=vs_plane_all[:].bitcast(U8).indirect(list4[:]))
-        vs_codes = sb.tile([P, N], U32, name="vs_codes", align_bytes=64)
-        nc.vector.tensor_copy(out=vs_codes[:], in_=vs_all[:].bitcast(U32).indirect(list4[:]))
-
-        for h in range(2):
-            partner = sb.tile([P, PACK, HALF], F32, name="partner%d" % h, tag=("partner", "w_codes")[h], align_bytes=64)
-            for t in range(PACK):
+        partner = sb.tile([P, PACK, J], F32, name="partner")
+        diff = sb.tile([P, 2, PACK, HALF], F32, name="diff")
+        for t in range(PACK):
+            for cols in halves if t == PACK - 1 else [all_slots]:
                 nc.scalar.activation(
-                    out=partner[:, t, :],
-                    in_=b_sb[t][:].indirect(list3[:, 8 * h : 8 * (h + 1)]),
+                    out=partner[:, t, cols],
+                    in_=b_sb[t][:].indirect(list3[:, cols.start // 16 : cols.stop // 16]),
                     func=ACT.Copy,
                     scale=sa_sb[:, t : t + 1],
                 )
-            hid = sb.tile([P, HALF * PACK], BF16, name="hid%d" % h, align_bytes=64)
-            diff = shared.tile([P, HALF * PACK], F32, name="diff%d" % h, offset=(3072, 1024)[h])
-            if h == 0:
                 nc.vector.tensor_tensor(
-                    out=diff[:].rearrange("p (c i t) -> p c t i", t=PACK, i=4),
-                    in0=a_ps[h][:].rearrange("p t (c i) -> p c t i", i=4),
-                    in1=partner[:].rearrange("p t (c i) -> p c t i", i=4),
+                    out=diff[:, cols.start // HALF : cols.stop // HALF, t, :],
+                    in0=a_ps[t][:, cols].rearrange("p (h j) -> p h j", j=HALF),
+                    in1=partner[:, t, cols].rearrange("p (h j) -> p h j", j=HALF),
                     op=ALU.subtract,
                 )
-                nc.scalar.activation(out=hid[:], in_=diff[:], func=ACT.Abs)
-            else:
-                for t in range(PACK):
-                    nc.vector.tensor_tensor(
-                        out=diff[:, HALF * t : HALF * (t + 1)],
-                        in0=a_ps[h][:, t, :],
-                        in1=partner[:, t, :],
-                        op=ALU.subtract,
-                    )
-                nc.scalar.activation(
-                    out=hid[:].rearrange("p (j t) -> p j t", t=PACK),
-                    in_=diff[:].rearrange("p (t j) -> p j t", t=PACK),
-                    func=ACT.Abs,
-                )
-            hid_codes = sb.tile([P, HALF], U32, name="hid_codes%d" % h, align_bytes=64)
-            hid_plane = sb.tile([P, HALF], U8, name="hid_plane%d" % h, align_bytes=64)
-            nc.vector.quantize_mx(out=hid_codes[:].bitcast(E5M2X4), scales=hid_plane[:], in_=hid[:])
+
+        hid = sb.tile([P, J, PACK], BF16, name="hid", align_bytes=64)
+        hid_codes, hid_plane = mx_tiles("hid", J)
+        for h, cols in enumerate(halves):
+            woven_diff = diff[:, h, :, :].rearrange("p t j -> p j t")
+            hid_half = hid[:, cols, :]
+            nc.scalar.activation(out=hid_half[:, 0:64, :], in_=woven_diff[:, 0:64, :], func=ACT.Abs)
+            nc.vector.scalar_tensor_tensor(
+                out=hid_half[:, 64:HALF, :],
+                in0=woven_diff[:, 64:HALF, :],
+                scalar=-1.0,
+                in1=woven_diff[:, 64:HALF, :],
+                op0=ALU.mult,
+                op1=ALU.max,
+            )
+            quantise(hid, hid_codes, hid_plane, cols, E5M2X4)
+        for h, cols in enumerate(halves):
             for m in range(2):
                 rows = slice(P * m, P * (m + 1))
                 y_ps = psum.tile([P, HALF], F32, name="y_ps%d%d" % (h, m), tag="bank%d" % (2 * h + m))
@@ -202,16 +214,15 @@ def tile_list_scaledpartner_twosteps_store_plain_kernel(
                     out=y_ps[:],
                     lhsT=vs_codes[:, rows].bitcast(E4M3X4),
                     lhsT_scale=vs_plane[:, rows],
-                    rhs=hid_codes[:].bitcast(E5M2X4),
-                    rhs_scale=hid_plane[:],
+                    rhs=hid_codes[:, cols].bitcast(E5M2X4),
+                    rhs_scale=hid_plane[:, cols],
                     start=True,
                     stop=True,
                 )
                 y_sb = sb.tile([P, HALF], F32, name="y_sb%d%d" % (h, m))
-                dst = out[rows, HALF * h : HALF * (h + 1)]
                 if m == 0:
                     nc.vector.tensor_copy(out=y_sb[:], in_=y_ps[:])
-                    nc.sync.dma_start(out=dst, in_=y_sb[:])
+                    nc.sync.dma_start(out=out[rows, cols], in_=y_sb[:])
                 else:
                     nc.scalar.copy(out=y_sb[:], in_=y_ps[:])
-                    nc.scalar.dma_start(out=dst, in_=y_sb[:])
+                    nc.scalar.dma_start(out=out[rows, cols], in_=y_sb[:])

from contextlib import ExitStack

import concourse.mybir as mybir

K, T, J, R, N, S = 512, 1024, 256, 512, 256, 1024
FLOPS = 2 * K * R * J * 2 + 2 * R * N * J

F32 = mybir.dt.float32
BF16 = mybir.dt.bfloat16
I32 = mybir.dt.int32
U32 = mybir.dt.uint32
U16 = mybir.dt.uint16
U8 = mybir.dt.uint8
E4M3X4 = mybir.dt.float8_e4m3fn_x4
E5M2X4 = mybir.dt.float8_e5m2_x4
ACT = mybir.ActivationFunctionType
ALU = mybir.AluOpType

P = 128
PACK = 4
HALF = J // 2
LIST_COLS = J // 16


def tile_list_scaledpartner_twosteps_store_plain_kernel(
    tc, cq, ga, gb, w_words, w_scales, sa, vs_words, vs_scales, offs, offs2, offs3, offs4, out
):
    nc = tc.nc
    with ExitStack() as ctx:
        sb = ctx.enter_context(tc.tile_pool(name="sb", bufs=1))
        shared = ctx.enter_context(tc.tile_pool(name="shared", bufs=1))
        psum = ctx.enter_context(tc.psum_pool(name="psum", bufs=1))

        def load_list(name, src):
            tile = sb.tile([P, LIST_COLS], U16, name=name)
            nc.sync.dma_start(out=tile[:], in_=src)
            return tile

        def load_row_factors(name, src, queue, lo=0, hi=PACK):
            tile = sb.tile([P, hi - lo], F32, name=name)
            queue.dma_start(out=tile[:], in_=src.rearrange("(p t) o -> p (t o)", t=PACK)[:, lo:hi])
            return tile

        def load_words(tile, src):
            nc.sync.dma_start(out=tile[:], in_=src[0].rearrange("p c t -> p (c t)").bitcast(I32))

        cq_rows = cq.rearrange("(p t) c -> p t c", t=PACK)
        cq_sb = [sb.tile([P, T], F32, name="cq%d" % t) for t in range(PACK)]

        nc.sync.dma_start(out=cq_sb[0][:], in_=cq_rows[:, 0, :])
        list2 = load_list("list2", offs2)
        list1 = load_list("list1", offs)
        gb_sb = load_row_factors("gb_sb", gb, nc.scalar)
        ga_early = load_row_factors("ga_early", ga, nc.scalar, 0, 2)
        w_staged = sb.tile([4, 4, R // 4], I32, name="w_staged")
        nc.scalar.dma_start(out=w_staged[:], in_=w_scales[0].bitcast(I32).rearrange("(q r) c -> r q c", r=4))
        warm_in = sb.tile([P, 1], F32, name="warm_in")
        nc.gpsimd.memset(warm_in[:], 0.0)
        warm_out = sb.tile([P, 1], F32, name="warm_out")
        nc.scalar.activation(out=warm_out[:], in_=warm_in[:], func=ACT.Abs)
        nc.sync.dma_start(out=cq_sb[1][:], in_=cq_rows[:, 1, :])
        nc.sync.dma_start(out=cq_sb[2][:], in_=cq_rows[:, 2, :])
        nc.sync.dma_start(out=cq_sb[3][:], in_=cq_rows[:, 3, :])
        ga_late = load_row_factors("ga_late", ga, nc.sync, 2, 4)
        w_raw = sb.tile([P, R], I32, name="w_raw")
        load_words(w_raw, w_words)
        w_plane_raw = sb.tile([P, R // 4], I32, name="w_plane_raw")
        nc.vector.memset(w_plane_raw[:], 0)
        vs_all = shared.tile([P, S], I32, name="vs_all", offset=0)
        vs_plane_all = sb.tile([P, S // 4], I32, name="vs_plane_all")
        nc.vector.memset(vs_plane_all[:], 0)
        list4 = load_list("list4", offs4)
        load_words(vs_all, vs_words)
        for q in range(4):
            nc.sync.dma_start(out=vs_plane_all[32 * q : 32 * q + 4, :], in_=vs_scales[0, 4 * q : 4 * q + 4, :].bitcast(I32))
        list3 = load_list("list3", offs3)
        sa_sb = load_row_factors("sa_sb", sa, nc.sync)
        for q in range(4):
            nc.vector.tensor_copy(out=w_plane_raw[32 * q : 32 * q + 4, :], in_=w_staged[:, q, :])

        w_plane = sb.tile([P, R], U8, name="w_plane", align_bytes=64)
        nc.vector.tensor_copy(
            out=w_plane[:].rearrange("p (t c i) -> p c t i", t=PACK, i=16),
            in_=w_plane_raw[:].bitcast(U8).rearrange("p (c i t) -> p c t i", t=PACK, i=16),
        )

        x1_rows = sb.tile([P, PACK, J], BF16, name="x1_rows")
        x2_rows = sb.tile([P, PACK, J], BF16, name="x2_rows")
        x1_woven = shared.tile([P, J, PACK], BF16, name="x1_woven", align_bytes=64, offset=5120)
        x2_woven = sb.tile([P, J, PACK], BF16, name="x2_woven", align_bytes=64)

        def fetch(rows, t, picks, step):
            nc.scalar.activation(out=rows[:, t, :], in_=cq_sb[t][:].indirect(picks[:]), func=ACT.Copy, scale=step)

        def weave(move, woven, rows, t0, cols):
            move(
                out=woven[:, cols, t0 : t0 + 2], in_=rows[:, t0 : t0 + 2, cols].rearrange("p t j -> p j t")
            )

        def quantise(woven, codes, plane, cols, fmt):
            nc.vector.quantize_mx(
                out=codes[:, cols].bitcast(fmt), scales=plane[:, cols], in_=woven[:, cols, :].rearrange("p j t -> p (j t)")
            )

        def mx_tiles(name, width):
            codes = sb.tile([P, width], U32, name=name + "_codes", align_bytes=64)
            plane = sb.tile([P, width], U8, name=name + "_plane", align_bytes=64)
            return codes, plane

        halves = [slice(HALF * h, HALF * (h + 1)) for h in range(2)]
        all_slots = slice(0, J)
        for t in range(2):
            fetch(x2_rows, t, list2, gb_sb[:, t : t + 1])
            fetch(x1_rows, t, list1, ga_early[:, t : t + 1])
        weave(nc.vector.tensor_copy, x2_woven, x2_rows, 0, all_slots)
        weave(nc.vector.tensor_copy, x1_woven, x1_rows, 0, all_slots)
        for t in range(2, 4):
            fetch(x2_rows, t, list2, gb_sb[:, t : t + 1])
        for t in range(2, 4):
            fetch(x1_rows, t, list1, ga_late[:, t - 2 : t - 1])
        w_codes = sb.tile([P, R], I32, name="w_codes", tag="w_codes", align_bytes=64)

        def deal_w(lo, hi):
            nc.vector.tensor_copy(
                out=w_codes[:].rearrange("p (t c i) -> p c t i", t=PACK, i=4)[:, :, lo:hi, :],
                in_=w_raw[:].rearrange("p (c i t) -> p c t i", t=PACK, i=4)[:, :, lo:hi, :],
            )

        def times_w(acc, t, codes, plane):
            cols = slice(P * t, P * (t + 1))
            nc.tensor.matmul_mx(
                out=acc,
                lhsT=w_codes[:, cols].bitcast(E5M2X4),
                lhsT_scale=w_plane[:, cols],
                rhs=codes.bitcast(E4M3X4),
                rhs_scale=plane,
                start=True,
                stop=True,
            )

        x2_codes, x2_plane = mx_tiles("x2", J)
        for cols in halves:
            weave(nc.vector.tensor_copy, x2_woven, x2_rows, 2, cols)
        deal_w(0, 1)
        for cols in halves:
            quantise(x2_woven, x2_codes, x2_plane, cols, E4M3X4)
        deal_w(1, PACK)

        vs_codes = sb.tile([P, N], U32, name="vs_codes", align_bytes=64)
        nc.vector.tensor_copy(out=vs_codes[:], in_=vs_all[:].bitcast(U32).indirect(list4[:]))
        vs_plane = sb.tile([P, N], U8, name="vs_plane", align_bytes=64)
        nc.vector.tensor_copy(out=vs_plane[:], in_=vs_plane_all[:].bitcast(U8).indirect(list4[:]))

        weave(nc.scalar.copy, x1_woven, x1_rows, 2, halves[0])
        weave(nc.vector.tensor_copy, x1_woven, x1_rows, 2, halves[1])
        x1_codes = shared.tile([P, J], U32, name="x1_codes", align_bytes=64, offset=0)
        x1_plane = sb.tile([P, J], U8, name="x1_plane", align_bytes=64)

        b_sb = []
        for t in range(PACK):
            b_ps = psum.tile([P, J], F32, name="b_ps%d" % t, tag="bank%d" % t)
            for cols in halves:
                times_w(b_ps[:, cols], t, x2_codes[:, cols], x2_plane[:, cols])
            b_t = shared.tile([P, J if t == PACK - 1 else 2 * J], F32, name="b_sb%d" % t, offset=(8192, 3072, 6144, 1024)[t])
            if t == 0:
                nc.scalar.copy(out=b_t[:, 0:J], in_=b_ps[:])
            else:
                nc.vector.tensor_copy(out=b_t[:, 0:J], in_=b_ps[:])
            if t == 1:
                quantise(x1_woven, x1_codes, x1_plane, all_slots, E4M3X4)
            b_sb.append(b_t)

        a_ps = [psum.tile([P, J], F32, name="a_ps%d" % t) for t in range(PACK)]
        for t in range(PACK):
            times_w(a_ps[t][:], t, x1_codes[:], x1_plane[:])

        partner = sb.tile([P, PACK, J], F32, name="partner")
        diff = sb.tile([P, 2, PACK, HALF], F32, name="diff")
        for t in range(PACK):
            for cols in halves if t == PACK - 1 else [all_slots]:
                nc.scalar.activation(
                    out=partner[:, t, cols],
                    in_=b_sb[t][:].indirect(list3[:, cols.start // 16 : cols.stop // 16]),
                    func=ACT.Copy,
                    scale=sa_sb[:, t : t + 1],
                )
                nc.vector.tensor_tensor(
                    out=diff[:, cols.start // HALF : cols.stop // HALF, t, :],
                    in0=a_ps[t][:, cols].rearrange("p (h j) -> p h j", j=HALF),
                    in1=partner[:, t, cols].rearrange("p (h j) -> p h j", j=HALF),
                    op=ALU.subtract,
                )

        hid = sb.tile([P, J, PACK], BF16, name="hid", align_bytes=64)
        hid_codes, hid_plane = mx_tiles("hid", J)
        for h, cols in enumerate(halves):
            woven_diff = diff[:, h, :, :].rearrange("p t j -> p j t")
            hid_half = hid[:, cols, :]
            nc.scalar.activation(out=hid_half[:, 0:64, :], in_=woven_diff[:, 0:64, :], func=ACT.Abs)
            nc.vector.scalar_tensor_tensor(
                out=hid_half[:, 64:HALF, :],
                in0=woven_diff[:, 64:HALF, :],
                scalar=-1.0,
                in1=woven_diff[:, 64:HALF, :],
                op0=ALU.mult,
                op1=ALU.max,
            )
            quantise(hid, hid_codes, hid_plane, cols, E5M2X4)
        for h, cols in enumerate(halves):
            for m in range(2):
                rows = slice(P * m, P * (m + 1))
                y_ps = psum.tile([P, HALF], F32, name="y_ps%d%d" % (h, m), tag="bank%d" % (2 * h + m))
                nc.tensor.matmul_mx(
                    out=y_ps[:],
                    lhsT=vs_codes[:, rows].bitcast(E4M3X4),
                    lhsT_scale=vs_plane[:, rows],
                    rhs=hid_codes[:, cols].bitcast(E5M2X4),
                    rhs_scale=hid_plane[:, cols],
                    start=True,
                    stop=True,
                )
                y_sb = sb.tile([P, HALF], F32, name="y_sb%d%d" % (h, m))
                if m == 0:
                    nc.vector.tensor_copy(out=y_sb[:], in_=y_ps[:])
                    nc.sync.dma_start(out=out[rows, cols], in_=y_sb[:])
                else:
                    nc.scalar.copy(out=y_sb[:], in_=y_ps[:])
                    nc.scalar.dma_start(out=out[rows, cols], in_=y_sb[:])
